import numpy as np
import ml_dtypes


def mxq(x, axis, fmt="e4m3"):
    dtype, down = {"e4m3": (ml_dtypes.float8_e4m3fn, 7), "e5m2": (ml_dtypes.float8_e5m2, 14)}[fmt]
    v = np.moveaxis(np.asarray(x, np.float32).astype(ml_dtypes.bfloat16).astype(np.float64), axis, -1)
    blocks = v.reshape(v.shape[:-1] + (-1, 32))
    amax = np.abs(blocks).max(-1, keepdims=True)
    byte = np.maximum(np.where(amax > 0, np.frexp(amax)[1] - 1 + 127, 0) - down, 1)
    scale = np.exp2(byte - 127.0)
    codes = (blocks / scale).astype(np.float32).astype(dtype).astype(np.float64)
    return np.moveaxis((codes * scale).reshape(v.shape), -1, axis)


WIDE = False


def mx_kscale(k):
    if not WIDE:
        return np.ones(k)
    levels = np.array([10, -10, 5, -5, 0])
    if k % 512:
        return np.exp2(np.random.permutation(np.resize(levels, k // 32))).repeat(32)
    a = np.empty((k // 512, 16))
    for p in range(k // 512):
        a[p, :8] = np.random.permutation(np.resize(levels, 8))
        for g in range(8):
            far = levels[np.abs(levels - a[p, g]) >= 10]
            a[p, g + 8] = far[np.random.randint(len(far))]
    return np.exp2(a.ravel()).repeat(32)


def f64(x):
    return np.asarray(x).astype(np.float64)


def striped(idx):
    return np.tile(idx.reshape(-1, 16).T, (8, 1)).astype(np.uint16)


def unstriped(offs):
    return offs[:16].T.reshape(-1).astype(np.int64)


K, T, D, S, V, N = 512, 2048, 4, 512, 128, 128


def setup_inputs():
    n = np.random.standard_normal
    s = mx_kscale(K)[:, None]
    return {
        "xT": (n((K, T)) * s).astype(np.float32),
        "w": (n((K, N)) / np.sqrt(K) / s).astype(np.float32),
        "b": (0.3 * n((N, 1))).astype(np.float32),
        "offs": striped(np.random.permutation(T)[:S]),
    }


def reference(xT, w, b, offs):
    idx = unstriped(offs)
    xq = mxq(f64(xT)[:, idx], 0, "e4m3")
    y = mxq(f64(w), 0, "e4m3").T @ xq
    y = y + f64(b)
    return y.reshape(N, V, D).max(axis=2)

@@ -1,0 +1,100 @@
+from contextlib import ExitStack
+
+import concourse.mybir as mybir
+
+K, T, S, N, D = 512, 2048, 512, 128, 4
+V = S // D
+P = 128
+PACK = 4
+HALF = S // 2
+CHUNKS = ((0, 1024), (1024, 1664), (1664, 2048))
+FLOPS = 2 * K * S * N
+
+F32 = mybir.dt.float32
+BF16 = mybir.dt.bfloat16
+U16 = mybir.dt.uint16
+U32 = mybir.dt.uint32
+U8 = mybir.dt.uint8
+FP8X4 = mybir.dt.float8_e4m3fn_x4
+MAX = mybir.AluOpType.max
+X = mybir.AxisListType.X
+IDENTITY = mybir.ActivationFunctionType.Identity
+COPY = mybir.ActivationFunctionType.Copy
+
+
+def tile_picked_pool_lin_bias_sub_e_kernel(tc, xT, w, b, offs, out):
+    nc = tc.nc
+    with ExitStack() as ctx:
+        keep = ctx.enter_context(tc.tile_pool(name="keep", bufs=1))
+        psum = ctx.enter_context(tc.psum_pool(name="psum", bufs=1))
+
+        offsets = keep.tile([P, S // 16], U16, name="offsets")
+        nc.sync.dma_start(offsets[:], offs)
+
+        xT_rows = xT.rearrange("(p j) t -> p j t", j=PACK)
+        planes = []
+        for j in range(PACK):
+            plane = keep.tile([P, T], F32, name="plane%d" % j)
+            for lo, hi in ([(0, T)] if j < PACK - 1 else CHUNKS):
+                nc.sync.dma_start(plane[:, lo:hi], xT_rows[:, j, lo:hi])
+            planes.append(plane)
+        w_raw = keep.tile([P, PACK, N], F32, name="w_raw")
+        nc.sync.dma_start(w_raw[:], w.rearrange("(p j) n -> p j n", j=PACK))
+        bias = keep.tile([P, 1], F32, name="bias")
+        nc.sync.dma_start(bias[:], b)
+
+        halves = []
+        for h in range(2):
+            halves.append(keep.tile([P, HALF, PACK], BF16, name="picked%d" % h, align_bytes=64))
+        for j in range(PACK - 1):
+            for h in range(2):
+                lo = h * (HALF // 16)
+                nc.vector.tensor_copy(halves[h][:, :, j], planes[j][:].indirect(offsets[:, lo : lo + HALF // 16]))
+        last = keep.tile([P, T], BF16, name="last")
+        nc.scalar.copy(last[:, 0:1024], planes[3][:, 0:1024])
+        nc.vector.tensor_copy(last[:, 1024:1664], planes[3][:, 1024:1664])
+        nc.vector.tensor_copy(last[:, 1664:2048], planes[3][:, 1664:2048])
+        nc.vector.tensor_copy(halves[1][:, :, 3], planes[3][:].indirect(offsets[:, HALF // 16 : S // 16]))
+        nc.scalar.activation(halves[0][:, :, 3], last[:].indirect(offsets[:, 0 : HALF // 16]), COPY)
+
+        w_grouped = keep.tile([P, N, PACK], BF16, name="w_grouped", align_bytes=64)
+        nc.gpsimd.tensor_scalar(w_grouped[:], w_raw[:].rearrange("p j n -> p n j"), 1.0, 0.0, mybir.AluOpType.mult, mybir.AluOpType.add)
+        w_codes = keep.tile([P, N], U32, name="w_codes", align_bytes=64)
+        w_scales = keep.tile([P, N], U8, name="w_scales", align_bytes=64)
+        nc.vector.quantize_mx(
+            out=w_codes[:].bitcast(FP8X4),
+            scales=w_scales[:],
+            in_=w_grouped[:].rearrange("p n j -> p (n j)"),
+        )
+
+        codes, scales = {}, {}
+        for h in (1, 0):
+            c = keep.tile([P, HALF], U32, name="codes%d" % h, align_bytes=64)
+            s = keep.tile([P, HALF], U8, name="scales%d" % h, align_bytes=64)
+            nc.vector.quantize_mx(
+                out=c[:].bitcast(FP8X4),
+                scales=s[:],
+                in_=halves[h][:].rearrange("p t j -> p (t j)"),
+            )
+            codes[h] = c
+            scales[h] = s
+
+        for h in (1, 0):
+            acc = psum.tile([P, HALF], F32, name="acc%d" % h)
+            nc.tensor.matmul_mx(
+                out=acc[:],
+                lhsT=w_codes[:].bitcast(FP8X4),
+                lhsT_scale=w_scales[:],
+                rhs=codes[h][:].bitcast(FP8X4),
+                rhs_scale=scales[h][:],
+                start=True,
+                stop=True,
+            )
+            best = keep.tile([P, HALF // D], F32, name="best%d" % h, tag="picked0" if h == 1 else "best", align_bytes=64)
+            nc.vector.tensor_reduce(best[:], acc[:].rearrange("m (v d) -> m v d", d=D), axis=X, op=MAX)
+            result = keep.tile([P, HALF // D], F32, name="result%d" % h)
+            if h == 1:
+                nc.scalar.activation(result[:], best[:], IDENTITY, bias=bias[:, 0:1])
+            else:
+                nc.vector.tensor_scalar_add(result[:], best[:], bias[:, 0:1])
+            nc.sync.dma_start(out[:, h * (HALF // D) : (h + 1) * (HALF // D)], result[:])

@@ -7,7 +7,8 @@ V = S // D
 P = 128
 PACK = 4
 HALF = S // 2
-CHUNKS = ((0, 1024), (1024, 1664), (1664, 2048))
+QUARTER = S // 4
+CHUNKS = ((0, 896), (896, 1536), (1536, 1856), (1856, 2048))
 FLOPS = 2 * K * S * N
 
 F32 = mybir.dt.float32
@@ -29,7 +30,6 @@ def tile_picked_pool_lin_bias_sub_e_kernel(tc, xT, w, b, offs, out):
         psum = ctx.enter_context(tc.psum_pool(name="psum", bufs=1))
 
         offsets = keep.tile([P, S // 16], U16, name="offsets")
-        nc.sync.dma_start(offsets[:], offs)
 
         xT_rows = xT.rearrange("(p j) t -> p j t", j=PACK)
         planes = []
@@ -38,6 +38,8 @@ def tile_picked_pool_lin_bias_sub_e_kernel(tc, xT, w, b, offs, out):
             for lo, hi in ([(0, T)] if j < PACK - 1 else CHUNKS):
                 nc.sync.dma_start(plane[:, lo:hi], xT_rows[:, j, lo:hi])
             planes.append(plane)
+            if j == 0:
+                nc.sync.dma_start(offsets[:], offs)
         w_raw = keep.tile([P, PACK, N], F32, name="w_raw")
         nc.sync.dma_start(w_raw[:], w.rearrange("(p j) n -> p j n", j=PACK))
         bias = keep.tile([P, 1], F32, name="bias")
@@ -51,9 +53,11 @@ def tile_picked_pool_lin_bias_sub_e_kernel(tc, xT, w, b, offs, out):
                 lo = h * (HALF // 16)
                 nc.vector.tensor_copy(halves[h][:, :, j], planes[j][:].indirect(offsets[:, lo : lo + HALF // 16]))
         last = keep.tile([P, T], BF16, name="last")
-        nc.scalar.copy(last[:, 0:1024], planes[3][:, 0:1024])
-        nc.vector.tensor_copy(last[:, 1024:1664], planes[3][:, 1024:1664])
-        nc.vector.tensor_copy(last[:, 1664:2048], planes[3][:, 1664:2048])
+        for c, (lo, hi) in enumerate(CHUNKS):
+            if c in (0, len(CHUNKS) - 1):
+                nc.scalar.copy(last[:, lo:hi], planes[3][:, lo:hi])
+            else:
+                nc.vector.tensor_copy(last[:, lo:hi], planes[3][:, lo:hi])
         nc.vector.tensor_copy(halves[1][:, :, 3], planes[3][:].indirect(offsets[:, HALF // 16 : S // 16]))
         nc.scalar.activation(halves[0][:, :, 3], last[:].indirect(offsets[:, 0 : HALF // 16]), COPY)
 
@@ -67,34 +71,41 @@ def tile_picked_pool_lin_bias_sub_e_kernel(tc, xT, w, b, offs, out):
             in_=w_grouped[:].rearrange("p n j -> p (n j)"),
         )
 
+        order = (2, 3, 0, 1)
         codes, scales = {}, {}
-        for h in (1, 0):
-            c = keep.tile([P, HALF], U32, name="codes%d" % h, align_bytes=64)
-            s = keep.tile([P, HALF], U8, name="scales%d" % h, align_bytes=64)
+        for q in order:
+            c = keep.tile([P, QUARTER], U32, name="codes%d" % q, align_bytes=64)
+            s = keep.tile([P, QUARTER], U8, name="scales%d" % q, align_bytes=64)
+            lo = (q % 2) * QUARTER
             nc.vector.quantize_mx(
                 out=c[:].bitcast(FP8X4),
                 scales=s[:],
-                in_=halves[h][:].rearrange("p t j -> p (t j)"),
+                in_=halves[q // 2][:, lo : lo + QUARTER, :].rearrange("p t j -> p (t j)"),
             )
-            codes[h] = c
-            scales[h] = s
+            codes[q] = c
+            scales[q] = s
 
+        width = QUARTER // D
         for h in (1, 0):
-            acc = psum.tile([P, HALF], F32, name="acc%d" % h)
-            nc.tensor.matmul_mx(
-                out=acc[:],
-                lhsT=w_codes[:].bitcast(FP8X4),
-                lhsT_scale=w_scales[:],
-                rhs=codes[h][:].bitcast(FP8X4),
-                rhs_scale=scales[h][:],
-                start=True,
-                stop=True,
-            )
-            best = keep.tile([P, HALF // D], F32, name="best%d" % h, tag="picked0" if h == 1 else "best", align_bytes=64)
-            nc.vector.tensor_reduce(best[:], acc[:].rearrange("m (v d) -> m v d", d=D), axis=X, op=MAX)
-            result = keep.tile([P, HALF // D], F32, name="result%d" % h)
+            best = keep.tile([P, 2 * width], F32, name="best%d" % h, tag="picked0" if h == 1 else "best", align_bytes=64)
+            for i in range(2):
+                q = 2 * h + i
+                acc = psum.tile([P, QUARTER], F32, name="acc%d" % q)
+                nc.tensor.matmul_mx(
+                    out=acc[:],
+                    lhsT=w_codes[:].bitcast(FP8X4),
+                    lhsT_scale=w_scales[:],
+                    rhs=codes[q][:].bitcast(FP8X4),
+                    rhs_scale=scales[q][:],
+                    start=True,
+                    stop=True,
+                )
+                nc.vector.tensor_reduce(
+                    best[:, i * width : (i + 1) * width], acc[:].rearrange("m (v d) -> m v d", d=D), axis=X, op=MAX
+                )
+            result = keep.tile([P, 2 * width], F32, name="result%d" % h)
             if h == 1:
                 nc.scalar.activation(result[:], best[:], IDENTITY, bias=bias[:, 0:1])
             else:
                 nc.vector.tensor_scalar_add(result[:], best[:], bias[:, 0:1])
-            nc.sync.dma_start(out[:, h * (HALF // D) : (h + 1) * (HALF // D)], result[:])
+            nc.sync.dma_start(out[:, h * 2 * width : (h + 1) * 2 * width], result[:])

@@ -40,7 +40,7 @@ def tile_picked_pool_lin_bias_sub_e_kernel(tc, xT, w, b, offs, out):
             planes.append(plane)
             if j == 0:
                 nc.sync.dma_start(offsets[:], offs)
-        w_raw = keep.tile([P, PACK, N], F32, name="w_raw")
+        w_raw = keep.tile([P, PACK, N], F32, name="w_raw", align_bytes=64)
         nc.sync.dma_start(w_raw[:], w.rearrange("(p j) n -> p j n", j=PACK))
         bias = keep.tile([P, 1], F32, name="bias")
         nc.sync.dma_start(bias[:], b)
@@ -73,13 +73,15 @@ def tile_picked_pool_lin_bias_sub_e_kernel(tc, xT, w, b, offs, out):
 
         order = (2, 3, 0, 1)
         codes, scales = {}, {}
-        for q in order:
+        first_scales = keep.tile([P, QUARTER], U8, name="first_scales", align_bytes=64)
+        later_scales = keep.tile([P, 3 * QUARTER], U8, name="later_scales", tag="w_raw", align_bytes=64)
+        for i, q in enumerate(order):
             c = keep.tile([P, QUARTER], U32, name="codes%d" % q, align_bytes=64)
-            s = keep.tile([P, QUARTER], U8, name="scales%d" % q, align_bytes=64)
+            s = first_scales[:] if i == 0 else later_scales[:, (i - 1) * QUARTER : i * QUARTER]
             lo = (q % 2) * QUARTER
             nc.vector.quantize_mx(
                 out=c[:].bitcast(FP8X4),
-                scales=s[:],
+                scales=s,
                 in_=halves[q // 2][:, lo : lo + QUARTER, :].rearrange("p t j -> p (t j)"),
             )
             codes[q] = c
@@ -96,7 +98,7 @@ def tile_picked_pool_lin_bias_sub_e_kernel(tc, xT, w, b, offs, out):
                     lhsT=w_codes[:].bitcast(FP8X4),
                     lhsT_scale=w_scales[:],
                     rhs=codes[q][:].bitcast(FP8X4),
-                    rhs_scale=scales[q][:],
+                    rhs_scale=scales[q],
                     start=True,
                     stop=True,
                 )

@@ -8,7 +8,7 @@ P = 128
 PACK = 4
 HALF = S // 2
 QUARTER = S // 4
-CHUNKS = ((0, 896), (896, 1536), (1536, 1856), (1856, 2048))
+CHUNKS = ((0, 896), (896, 1408), (1408, 1728), (1728, 2048))
 FLOPS = 2 * K * S * N
 
 F32 = mybir.dt.float32
@@ -34,7 +34,7 @@ def tile_picked_pool_lin_bias_sub_e_kernel(tc, xT, w, b, offs, out):
         xT_rows = xT.rearrange("(p j) t -> p j t", j=PACK)
         planes = []
         for j in range(PACK):
-            plane = keep.tile([P, T], F32, name="plane%d" % j)
+            plane = keep.tile([P, T], F32, name="plane%d" % j, align_bytes=64)
             for lo, hi in ([(0, T)] if j < PACK - 1 else CHUNKS):
                 nc.sync.dma_start(plane[:, lo:hi], xT_rows[:, j, lo:hi])
             planes.append(plane)
@@ -62,7 +62,10 @@ def tile_picked_pool_lin_bias_sub_e_kernel(tc, xT, w, b, offs, out):
         nc.scalar.activation(halves[0][:, :, 3], last[:].indirect(offsets[:, 0 : HALF // 16]), COPY)
 
         w_grouped = keep.tile([P, N, PACK], BF16, name="w_grouped", align_bytes=64)
-        nc.gpsimd.tensor_scalar(w_grouped[:], w_raw[:].rearrange("p j n -> p n j"), 1.0, 0.0, mybir.AluOpType.mult, mybir.AluOpType.add)
+        nc.vector.tensor_copy(
+            w_grouped[:].rearrange("p (c i) j -> p c j i", i=4),
+            w_raw[:].rearrange("p j (c i) -> p c j i", i=4),
+        )
         w_codes = keep.tile([P, N], U32, name="w_codes", align_bytes=64)
         w_scales = keep.tile([P, N], U8, name="w_scales", align_bytes=64)
         nc.vector.quantize_mx(
@@ -73,7 +76,7 @@ def tile_picked_pool_lin_bias_sub_e_kernel(tc, xT, w, b, offs, out):
 
         order = (2, 3, 0, 1)
         codes, scales = {}, {}
-        first_scales = keep.tile([P, QUARTER], U8, name="first_scales", align_bytes=64)
+        first_scales = keep.tile([P, QUARTER], U8, name="first_scales", tag="plane3", align_bytes=64)
         later_scales = keep.tile([P, 3 * QUARTER], U8, name="later_scales", tag="w_raw", align_bytes=64)
         for i, q in enumerate(order):
             c = keep.tile([P, QUARTER], U32, name="codes%d" % q, align_bytes=64)
@@ -89,7 +92,7 @@ def tile_picked_pool_lin_bias_sub_e_kernel(tc, xT, w, b, offs, out):
 
         width = QUARTER // D
         for h in (1, 0):
-            best = keep.tile([P, 2 * width], F32, name="best%d" % h, tag="picked0" if h == 1 else "best", align_bytes=64)
+            best = keep.tile([P, 2 * width], F32, name="best%d" % h, tag="last" if h == 1 else "best0")
             for i in range(2):
                 q = 2 * h + i
                 acc = psum.tile([P, QUARTER], F32, name="acc%d" % q)

@@ -8,7 +8,7 @@ P = 128
 PACK = 4
 HALF = S // 2
 QUARTER = S // 4
-CHUNKS = ((0, 896), (896, 1408), (1408, 1728), (1728, 2048))
+CHUNKS = ((0, 896), (896, 1536), (1536, 1856), (1856, 2048))
 FLOPS = 2 * K * S * N
 
 F32 = mybir.dt.float32

@@ -8,7 +8,7 @@ P = 128
 PACK = 4
 HALF = S // 2
 QUARTER = S // 4
-CHUNKS = ((0, 896), (896, 1536), (1536, 1856), (1856, 2048))
+CHUNKS = ((0, 960), (960, 1600), (1600, 1920), (1920, 2048))
 FLOPS = 2 * K * S * N
 
 F32 = mybir.dt.float32
@@ -35,8 +35,12 @@ def tile_picked_pool_lin_bias_sub_e_kernel(tc, xT, w, b, offs, out):
         planes = []
         for j in range(PACK):
             plane = keep.tile([P, T], F32, name="plane%d" % j, align_bytes=64)
-            for lo, hi in ([(0, T)] if j < PACK - 1 else CHUNKS):
-                nc.sync.dma_start(plane[:, lo:hi], xT_rows[:, j, lo:hi])
+            if j < PACK - 1:
+                nc.sync.dma_start(plane[0:P:2, :], xT_rows[0:P:2, j, :])
+                nc.scalar.dma_start(plane[1:P:2, :], xT_rows[1:P:2, j, :])
+            else:
+                for lo, hi in CHUNKS:
+                    nc.sync.dma_start(plane[:, lo:hi], xT_rows[:, j, lo:hi])
             planes.append(plane)
             if j == 0:
                 nc.sync.dma_start(offsets[:], offs)

@@ -34,7 +34,7 @@ def tile_picked_pool_lin_bias_sub_e_kernel(tc, xT, w, b, offs, out):
         xT_rows = xT.rearrange("(p j) t -> p j t", j=PACK)
         planes = []
         for j in range(PACK):
-            plane = keep.tile([P, T], F32, name="plane%d" % j, align_bytes=64)
+            plane = keep.tile([P, T], F32, name="plane%d" % j, align_bytes=256)
             if j < PACK - 1:
                 nc.sync.dma_start(plane[0:P:2, :], xT_rows[0:P:2, j, :])
                 nc.scalar.dma_start(plane[1:P:2, :], xT_rows[1:P:2, j, :])
@@ -44,7 +44,7 @@ def tile_picked_pool_lin_bias_sub_e_kernel(tc, xT, w, b, offs, out):
             planes.append(plane)
             if j == 0:
                 nc.sync.dma_start(offsets[:], offs)
-        w_raw = keep.tile([P, PACK, N], F32, name="w_raw", align_bytes=64)
+        w_raw = keep.tile([P, PACK, N], F32, name="w_raw", align_bytes=256)
         nc.sync.dma_start(w_raw[:], w.rearrange("(p j) n -> p j n", j=PACK))
         bias = keep.tile([P, 1], F32, name="bias")
         nc.sync.dma_start(bias[:], b)
@@ -80,8 +80,8 @@ def tile_picked_pool_lin_bias_sub_e_kernel(tc, xT, w, b, offs, out):
 
         order = (2, 3, 0, 1)
         codes, scales = {}, {}
-        first_scales = keep.tile([P, QUARTER], U8, name="first_scales", tag="plane3", align_bytes=64)
-        later_scales = keep.tile([P, 3 * QUARTER], U8, name="later_scales", tag="w_raw", align_bytes=64)
+        first_scales = keep.tile([P, QUARTER], U8, name="first_scales", tag="plane3", align_bytes=256)
+        later_scales = keep.tile([P, 3 * QUARTER], U8, name="later_scales", tag="w_raw", align_bytes=256)
         for i, q in enumerate(order):
             c = keep.tile([P, QUARTER], U32, name="codes%d" % q, align_bytes=64)
             s = first_scales[:] if i == 0 else later_scales[:, (i - 1) * QUARTER : i * QUARTER]

@@ -51,12 +51,12 @@ def tile_picked_pool_lin_bias_sub_e_kernel(tc, xT, w, b, offs, out):
 
         halves = []
         for h in range(2):
-            halves.append(keep.tile([P, HALF, PACK], BF16, name="picked%d" % h, align_bytes=64))
+            halves.append(keep.tile([P, HALF, PACK], BF16, name="picked%d" % h, align_bytes=256))
         for j in range(PACK - 1):
             for h in range(2):
                 lo = h * (HALF // 16)
                 nc.vector.tensor_copy(halves[h][:, :, j], planes[j][:].indirect(offsets[:, lo : lo + HALF // 16]))
-        last = keep.tile([P, T], BF16, name="last")
+        last = keep.tile([P, T], BF16, name="last", align_bytes=256)
         for c, (lo, hi) in enumerate(CHUNKS):
             if c in (0, len(CHUNKS) - 1):
                 nc.scalar.copy(last[:, lo:hi], planes[3][:, lo:hi])
@@ -65,13 +65,13 @@ def tile_picked_pool_lin_bias_sub_e_kernel(tc, xT, w, b, offs, out):
         nc.vector.tensor_copy(halves[1][:, :, 3], planes[3][:].indirect(offsets[:, HALF // 16 : S // 16]))
         nc.scalar.activation(halves[0][:, :, 3], last[:].indirect(offsets[:, 0 : HALF // 16]), COPY)
 
-        w_grouped = keep.tile([P, N, PACK], BF16, name="w_grouped", align_bytes=64)
+        w_grouped = keep.tile([P, N, PACK], BF16, name="w_grouped", align_bytes=256)
         nc.vector.tensor_copy(
             w_grouped[:].rearrange("p (c i) j -> p c j i", i=4),
             w_raw[:].rearrange("p j (c i) -> p c j i", i=4),
         )
-        w_codes = keep.tile([P, N], U32, name="w_codes", align_bytes=64)
-        w_scales = keep.tile([P, N], U8, name="w_scales", align_bytes=64)
+        w_codes = keep.tile([P, N], U32, name="w_codes", align_bytes=256)
+        w_scales = keep.tile([P, N], U8, name="w_scales", align_bytes=256)
         nc.vector.quantize_mx(
             out=w_codes[:].bitcast(FP8X4),
             scales=w_scales[:],
@@ -83,7 +83,7 @@ def tile_picked_pool_lin_bias_sub_e_kernel(tc, xT, w, b, offs, out):
         first_scales = keep.tile([P, QUARTER], U8, name="first_scales", tag="plane3", align_bytes=256)
         later_scales = keep.tile([P, 3 * QUARTER], U8, name="later_scales", tag="w_raw", align_bytes=256)
         for i, q in enumerate(order):
-            c = keep.tile([P, QUARTER], U32, name="codes%d" % q, align_bytes=64)
+            c = keep.tile([P, QUARTER], U32, name="codes%d" % q, align_bytes=256)
             s = first_scales[:] if i == 0 else later_scales[:, (i - 1) * QUARTER : i * QUARTER]
             lo = (q % 2) * QUARTER
             nc.vector.quantize_mx(
@@ -96,7 +96,7 @@ def tile_picked_pool_lin_bias_sub_e_kernel(tc, xT, w, b, offs, out):
 
         width = QUARTER // D
         for h in (1, 0):
-            best = keep.tile([P, 2 * width], F32, name="best%d" % h, tag="last" if h == 1 else "best0")
+            best = keep.tile([P, 2 * width], F32, name="best%d" % h, tag="last" if h == 1 else "best0", align_bytes=256)
             for i in range(2):
                 q = 2 * h + i
                 acc = psum.tile([P, QUARTER], F32, name="acc%d" % q)
@@ -112,7 +112,7 @@ def tile_picked_pool_lin_bias_sub_e_kernel(tc, xT, w, b, offs, out):
                 nc.vector.tensor_reduce(
                     best[:, i * width : (i + 1) * width], acc[:].rearrange("m (v d) -> m v d", d=D), axis=X, op=MAX
                 )
-            result = keep.tile([P, 2 * width], F32, name="result%d" % h)
+            result = keep.tile([P, 2 * width], F32, name="result%d" % h, align_bytes=256)
             if h == 1:
                 nc.scalar.activation(result[:], best[:], IDENTITY, bias=bias[:, 0:1])
             else:

@@ -8,7 +8,7 @@ P = 128
 PACK = 4
 HALF = S // 2
 QUARTER = S // 4
-CHUNKS = ((0, 960), (960, 1600), (1600, 1920), (1920, 2048))
+CHUNKS = ((0, 1024), (1024, 1664), (1664, 1920), (1920, 2048))
 FLOPS = 2 * K * S * N
 
 F32 = mybir.dt.float32

@@ -95,10 +95,11 @@ def tile_picked_pool_lin_bias_sub_e_kernel(tc, xT, w, b, offs, out):
             scales[q] = s
 
         width = QUARTER // D
-        for h in (1, 0):
-            best = keep.tile([P, 2 * width], F32, name="best%d" % h, tag="last" if h == 1 else "best0", align_bytes=256)
-            for i in range(2):
-                q = 2 * h + i
+        for first, count in ((2, 2), (0, 1), (1, 1)):
+            tag = "last" if first == 2 else "best%d" % first
+            best = keep.tile([P, count * width], F32, name="best%d" % first, tag=tag, align_bytes=256)
+            for i in range(count):
+                q = first + i
                 acc = psum.tile([P, QUARTER], F32, name="acc%d" % q)
                 nc.tensor.matmul_mx(
                     out=acc[:],
@@ -112,9 +113,10 @@ def tile_picked_pool_lin_bias_sub_e_kernel(tc, xT, w, b, offs, out):
                 nc.vector.tensor_reduce(
                     best[:, i * width : (i + 1) * width], acc[:].rearrange("m (v d) -> m v d", d=D), axis=X, op=MAX
                 )
-            result = keep.tile([P, 2 * width], F32, name="result%d" % h, align_bytes=256)
-            if h == 1:
-                nc.scalar.activation(result[:], best[:], IDENTITY, bias=bias[:, 0:1])
-            else:
+            result = keep.tile([P, count * width], F32, name="result%d" % first, align_bytes=256)
+            if first == 1:
                 nc.vector.tensor_scalar_add(result[:], best[:], bias[:, 0:1])
-            nc.sync.dma_start(out[:, h * 2 * width : (h + 1) * 2 * width], result[:])
+            else:
+                nc.scalar.activation(result[:], best[:], IDENTITY, bias=bias[:, 0:1])
+            queue = nc.scalar if first == 0 else nc.sync
+            queue.dma_start(out[:, first * width : (first + count) * width], result[:])

@@ -8,7 +8,7 @@ P = 128
 PACK = 4
 HALF = S // 2
 QUARTER = S // 4
-CHUNKS = ((0, 1024), (1024, 1664), (1664, 1920), (1920, 2048))
+CHUNKS = ((0, 800), (800, 1664), (1664, 1920), (1920, 2048))
 FLOPS = 2 * K * S * N
 
 F32 = mybir.dt.float32
@@ -57,11 +57,10 @@ def tile_picked_pool_lin_bias_sub_e_kernel(tc, xT, w, b, offs, out):
                 lo = h * (HALF // 16)
                 nc.vector.tensor_copy(halves[h][:, :, j], planes[j][:].indirect(offsets[:, lo : lo + HALF // 16]))
         last = keep.tile([P, T], BF16, name="last", align_bytes=256)
-        for c, (lo, hi) in enumerate(CHUNKS):
-            if c in (0, len(CHUNKS) - 1):
-                nc.scalar.copy(last[:, lo:hi], planes[3][:, lo:hi])
-            else:
-                nc.vector.tensor_copy(last[:, lo:hi], planes[3][:, lo:hi])
+        for lo, hi in (CHUNKS[0], (800, 1152), (1920, 1984)):
+            nc.scalar.copy(last[:, lo:hi], planes[3][:, lo:hi])
+        for lo, hi in ((1152, 1664), CHUNKS[2], (1984, 2048)):
+            nc.vector.tensor_copy(last[:, lo:hi], planes[3][:, lo:hi])
         nc.vector.tensor_copy(halves[1][:, :, 3], planes[3][:].indirect(offsets[:, HALF // 16 : S // 16]))
         nc.scalar.activation(halves[0][:, :, 3], last[:].indirect(offsets[:, 0 : HALF // 16]), COPY)
 

@@ -8,7 +8,7 @@ P = 128
 PACK = 4
 HALF = S // 2
 QUARTER = S // 4
-CHUNKS = ((0, 800), (800, 1664), (1664, 1920), (1920, 2048))
+CHUNKS = ((0, 832), (832, 1664), (1664, 1920), (1920, 2048))
 FLOPS = 2 * K * S * N
 
 F32 = mybir.dt.float32
@@ -57,25 +57,22 @@ def tile_picked_pool_lin_bias_sub_e_kernel(tc, xT, w, b, offs, out):
                 lo = h * (HALF // 16)
                 nc.vector.tensor_copy(halves[h][:, :, j], planes[j][:].indirect(offsets[:, lo : lo + HALF // 16]))
         last = keep.tile([P, T], BF16, name="last", align_bytes=256)
-        for lo, hi in (CHUNKS[0], (800, 1152), (1920, 1984)):
+        for lo, hi in (CHUNKS[0], (832, 1152), CHUNKS[3]):
             nc.scalar.copy(last[:, lo:hi], planes[3][:, lo:hi])
-        for lo, hi in ((1152, 1664), CHUNKS[2], (1984, 2048)):
+        for lo, hi in ((1152, 1664), CHUNKS[2]):
             nc.vector.tensor_copy(last[:, lo:hi], planes[3][:, lo:hi])
         nc.vector.tensor_copy(halves[1][:, :, 3], planes[3][:].indirect(offsets[:, HALF // 16 : S // 16]))
         nc.scalar.activation(halves[0][:, :, 3], last[:].indirect(offsets[:, 0 : HALF // 16]), COPY)
 
         w_grouped = keep.tile([P, N, PACK], BF16, name="w_grouped", align_bytes=256)
-        nc.vector.tensor_copy(
-            w_grouped[:].rearrange("p (c i) j -> p c j i", i=4),
-            w_raw[:].rearrange("p j (c i) -> p c j i", i=4),
-        )
+        w_halves = ((0, N // 2), (N // 2, N))
+        for lo, hi in w_halves:
+            nc.vector.tensor_copy(
+                w_grouped[:, lo:hi, :].rearrange("p (c i) j -> p c j i", i=4),
+                w_raw[:, :, lo:hi].rearrange("p j (c i) -> p c j i", i=4),
+            )
         w_codes = keep.tile([P, N], U32, name="w_codes", align_bytes=256)
         w_scales = keep.tile([P, N], U8, name="w_scales", align_bytes=256)
-        nc.vector.quantize_mx(
-            out=w_codes[:].bitcast(FP8X4),
-            scales=w_scales[:],
-            in_=w_grouped[:].rearrange("p n j -> p (n j)"),
-        )
 
         order = (2, 3, 0, 1)
         codes, scales = {}, {}
@@ -92,6 +89,13 @@ def tile_picked_pool_lin_bias_sub_e_kernel(tc, xT, w, b, offs, out):
             )
             codes[q] = c
             scales[q] = s
+            if i == 0:
+                for lo, hi in w_halves:
+                    nc.vector.quantize_mx(
+                        out=w_codes[:, lo:hi].bitcast(FP8X4),
+                        scales=w_scales[:, lo:hi],
+                        in_=w_grouped[:, lo:hi, :].rearrange("p n j -> p (n j)"),
+                    )
 
         width = QUARTER // D
         for first, count in ((2, 2), (0, 1), (1, 1)):

@@ -57,9 +57,9 @@ def tile_picked_pool_lin_bias_sub_e_kernel(tc, xT, w, b, offs, out):
                 lo = h * (HALF // 16)
                 nc.vector.tensor_copy(halves[h][:, :, j], planes[j][:].indirect(offsets[:, lo : lo + HALF // 16]))
         last = keep.tile([P, T], BF16, name="last", align_bytes=256)
-        for lo, hi in (CHUNKS[0], (832, 1152), CHUNKS[3]):
+        for lo, hi in (CHUNKS[0], (832, 1216), CHUNKS[3]):
             nc.scalar.copy(last[:, lo:hi], planes[3][:, lo:hi])
-        for lo, hi in ((1152, 1664), CHUNKS[2]):
+        for lo, hi in ((1216, 1664), CHUNKS[2]):
             nc.vector.tensor_copy(last[:, lo:hi], planes[3][:, lo:hi])
         nc.vector.tensor_copy(halves[1][:, :, 3], planes[3][:].indirect(offsets[:, HALF // 16 : S // 16]))
         nc.scalar.activation(halves[0][:, :, 3], last[:].indirect(offsets[:, 0 : HALF // 16]), COPY)

@@ -8,7 +8,6 @@ P = 128
 PACK = 4
 HALF = S // 2
 QUARTER = S // 4
-CHUNKS = ((0, 832), (832, 1664), (1664, 1920), (1920, 2048))
 FLOPS = 2 * K * S * N
 
 F32 = mybir.dt.float32
@@ -39,8 +38,7 @@ def tile_picked_pool_lin_bias_sub_e_kernel(tc, xT, w, b, offs, out):
                 nc.sync.dma_start(plane[0:P:2, :], xT_rows[0:P:2, j, :])
                 nc.scalar.dma_start(plane[1:P:2, :], xT_rows[1:P:2, j, :])
             else:
-                for lo, hi in CHUNKS:
-                    nc.sync.dma_start(plane[:, lo:hi], xT_rows[:, j, lo:hi])
+                nc.sync.dma_start(plane[:], xT_rows[:, j, :])
             planes.append(plane)
             if j == 0:
                 nc.sync.dma_start(offsets[:], offs)
@@ -52,17 +50,9 @@ def tile_picked_pool_lin_bias_sub_e_kernel(tc, xT, w, b, offs, out):
         halves = []
         for h in range(2):
             halves.append(keep.tile([P, HALF, PACK], BF16, name="picked%d" % h, align_bytes=256))
-        for j in range(PACK - 1):
-            for h in range(2):
-                lo = h * (HALF // 16)
-                nc.vector.tensor_copy(halves[h][:, :, j], planes[j][:].indirect(offsets[:, lo : lo + HALF // 16]))
-        last = keep.tile([P, T], BF16, name="last", align_bytes=256)
-        for lo, hi in (CHUNKS[0], (832, 1216), CHUNKS[3]):
-            nc.scalar.copy(last[:, lo:hi], planes[3][:, lo:hi])
-        for lo, hi in ((1216, 1664), CHUNKS[2]):
-            nc.vector.tensor_copy(last[:, lo:hi], planes[3][:, lo:hi])
-        nc.vector.tensor_copy(halves[1][:, :, 3], planes[3][:].indirect(offsets[:, HALF // 16 : S // 16]))
-        nc.scalar.activation(halves[0][:, :, 3], last[:].indirect(offsets[:, 0 : HALF // 16]), COPY)
+        for j in range(PACK):
+            nc.scalar.activation(halves[0][:, :, j], planes[j][:].indirect(offsets[:, 0 : HALF // 16]), COPY)
+            nc.vector.tensor_copy(halves[1][:, :, j], planes[j][:].indirect(offsets[:, HALF // 16 : S // 16]))
 
         w_grouped = keep.tile([P, N, PACK], BF16, name="w_grouped", align_bytes=256)
         w_halves = ((0, N // 2), (N // 2, N))
@@ -76,12 +66,18 @@ def tile_picked_pool_lin_bias_sub_e_kernel(tc, xT, w, b, offs, out):
 
         order = (2, 3, 0, 1)
         codes, scales = {}, {}
-        first_scales = keep.tile([P, QUARTER], U8, name="first_scales", tag="plane3", align_bytes=256)
-        later_scales = keep.tile([P, 3 * QUARTER], U8, name="later_scales", tag="w_raw", align_bytes=256)
+        all_scales = keep.tile([P, S], U8, name="all_scales", tag="w_raw", align_bytes=256)
         for i, q in enumerate(order):
             c = keep.tile([P, QUARTER], U32, name="codes%d" % q, align_bytes=256)
-            s = first_scales[:] if i == 0 else later_scales[:, (i - 1) * QUARTER : i * QUARTER]
+            s = all_scales[:, i * QUARTER : (i + 1) * QUARTER]
             lo = (q % 2) * QUARTER
+            if i == 0:
+                for wlo, whi in w_halves:
+                    nc.vector.quantize_mx(
+                        out=w_codes[:, wlo:whi].bitcast(FP8X4),
+                        scales=w_scales[:, wlo:whi],
+                        in_=w_grouped[:, wlo:whi, :].rearrange("p n j -> p (n j)"),
+                    )
             nc.vector.quantize_mx(
                 out=c[:].bitcast(FP8X4),
                 scales=s,
@@ -89,17 +85,10 @@ def tile_picked_pool_lin_bias_sub_e_kernel(tc, xT, w, b, offs, out):
             )
             codes[q] = c
             scales[q] = s
-            if i == 0:
-                for lo, hi in w_halves:
-                    nc.vector.quantize_mx(
-                        out=w_codes[:, lo:hi].bitcast(FP8X4),
-                        scales=w_scales[:, lo:hi],
-                        in_=w_grouped[:, lo:hi, :].rearrange("p n j -> p (n j)"),
-                    )
 
         width = QUARTER // D
         for first, count in ((2, 2), (0, 1), (1, 1)):
-            tag = "last" if first == 2 else "best%d" % first
+            tag = "picked0" if first == 2 else "best%d" % first
             best = keep.tile([P, count * width], F32, name="best%d" % first, tag=tag, align_bytes=256)
             for i in range(count):
                 q = first + i

@@ -35,7 +35,8 @@ def tile_picked_pool_lin_bias_sub_e_kernel(tc, xT, w, b, offs, out):
         for j in range(PACK):
             plane = keep.tile([P, T], F32, name="plane%d" % j, align_bytes=256)
             if j < PACK - 1:
-                nc.sync.dma_start(plane[0:P:2, :], xT_rows[0:P:2, j, :])
+                for lo in (0, T // 2):
+                    nc.sync.dma_start(plane[0:P:2, lo : lo + T // 2], xT_rows[0:P:2, j, lo : lo + T // 2])
                 nc.scalar.dma_start(plane[1:P:2, :], xT_rows[1:P:2, j, :])
             else:
                 nc.sync.dma_start(plane[:], xT_rows[:, j, :])

@@ -8,6 +8,7 @@ P = 128
 PACK = 4
 HALF = S // 2
 QUARTER = S // 4
+TAIL = 64
 FLOPS = 2 * K * S * N
 
 F32 = mybir.dt.float32
@@ -51,9 +52,24 @@ def tile_picked_pool_lin_bias_sub_e_kernel(tc, xT, w, b, offs, out):
         halves = []
         for h in range(2):
             halves.append(keep.tile([P, HALF, PACK], BF16, name="picked%d" % h, align_bytes=256))
-        for j in range(PACK):
-            nc.scalar.activation(halves[0][:, :, j], planes[j][:].indirect(offsets[:, 0 : HALF // 16]), COPY)
-            nc.vector.tensor_copy(halves[1][:, :, j], planes[j][:].indirect(offsets[:, HALF // 16 : S // 16]))
+        def entries(lo, hi):
+            return offsets[:, lo // 16 : hi // 16]
+
+        def scalar_gather(j, lo, hi):
+            h, at = divmod(lo, HALF)
+            nc.scalar.activation(halves[h][:, at : at + hi - lo, j], planes[j][:].indirect(entries(lo, hi)), COPY)
+
+        for j in range(2):
+            scalar_gather(j, 0, HALF)
+            nc.vector.tensor_copy(halves[1][:, :, j], planes[j][:].indirect(entries(HALF, S)))
+        staged = keep.tile([P, 2, TAIL], BF16, name="staged", align_bytes=256)
+        scalar_gather(2, 0, HALF)
+        scalar_gather(2, HALF, S - TAIL)
+        nc.vector.tensor_copy(staged[:, 0, :], planes[2][:].indirect(entries(S - TAIL, S)))
+        for lo in range(0, S - TAIL, QUARTER):
+            scalar_gather(3, lo, min(lo + QUARTER, S - TAIL))
+        nc.vector.tensor_copy(staged[:, 1, :], planes[3][:].indirect(entries(S - TAIL, S)))
+        nc.vector.tensor_copy(halves[1][:, HALF - TAIL :, 2:4], staged[:].rearrange("p j t -> p t j"))
 
         w_grouped = keep.tile([P, N, PACK], BF16, name="w_grouped", align_bytes=256)
         w_halves = ((0, N // 2), (N // 2, N))
@@ -65,7 +81,7 @@ def tile_picked_pool_lin_bias_sub_e_kernel(tc, xT, w, b, offs, out):
         w_codes = keep.tile([P, N], U32, name="w_codes", align_bytes=256)
         w_scales = keep.tile([P, N], U8, name="w_scales", align_bytes=256)
 
-        order = (2, 3, 0, 1)
+        order = (0, 1, 2, 3)
         codes, scales = {}, {}
         all_scales = keep.tile([P, S], U8, name="all_scales", tag="w_raw", align_bytes=256)
         for i, q in enumerate(order):
@@ -88,8 +104,8 @@ def tile_picked_pool_lin_bias_sub_e_kernel(tc, xT, w, b, offs, out):
             scales[q] = s
 
         width = QUARTER // D
-        for first, count in ((2, 2), (0, 1), (1, 1)):
-            tag = "picked0" if first == 2 else "best%d" % first
+        for first, count in ((0, 2), (2, 1), (3, 1)):
+            tag = "picked1" if first == 0 else "best%d" % first
             best = keep.tile([P, count * width], F32, name="best%d" % first, tag=tag, align_bytes=256)
             for i in range(count):
                 q = first + i
@@ -107,9 +123,9 @@ def tile_picked_pool_lin_bias_sub_e_kernel(tc, xT, w, b, offs, out):
                     best[:, i * width : (i + 1) * width], acc[:].rearrange("m (v d) -> m v d", d=D), axis=X, op=MAX
                 )
             result = keep.tile([P, count * width], F32, name="result%d" % first, align_bytes=256)
-            if first == 1:
+            if first == 3:
                 nc.vector.tensor_scalar_add(result[:], best[:], bias[:, 0:1])
             else:
                 nc.scalar.activation(result[:], best[:], IDENTITY, bias=bias[:, 0:1])
-            queue = nc.scalar if first == 0 else nc.sync
+            queue = nc.scalar if first == 2 else nc.sync
             queue.dma_start(out[:, first * width : (first + count) * width], result[:])

@@ -8,7 +8,7 @@ P = 128
 PACK = 4
 HALF = S // 2
 QUARTER = S // 4
-TAIL = 64
+V_LO, V_HI = 320, 384
 FLOPS = 2 * K * S * N
 
 F32 = mybir.dt.float32
@@ -49,27 +49,29 @@ def tile_picked_pool_lin_bias_sub_e_kernel(tc, xT, w, b, offs, out):
         bias = keep.tile([P, 1], F32, name="bias")
         nc.sync.dma_start(bias[:], b)
 
-        halves = []
-        for h in range(2):
-            halves.append(keep.tile([P, HALF, PACK], BF16, name="picked%d" % h, align_bytes=256))
+        gathered = keep.tile([P, S, PACK], BF16, name="gathered", align_bytes=256)
+
         def entries(lo, hi):
             return offsets[:, lo // 16 : hi // 16]
 
+        def picked(lo, hi):
+            return gathered[:, lo:hi, :]
+
         def scalar_gather(j, lo, hi):
-            h, at = divmod(lo, HALF)
-            nc.scalar.activation(halves[h][:, at : at + hi - lo, j], planes[j][:].indirect(entries(lo, hi)), COPY)
+            nc.scalar.activation(picked(lo, hi)[:, :, j], planes[j][:].indirect(entries(lo, hi)), COPY)
 
         for j in range(2):
             scalar_gather(j, 0, HALF)
-            nc.vector.tensor_copy(halves[1][:, :, j], planes[j][:].indirect(entries(HALF, S)))
-        staged = keep.tile([P, 2, TAIL], BF16, name="staged", align_bytes=256)
-        scalar_gather(2, 0, HALF)
-        scalar_gather(2, HALF, S - TAIL)
-        nc.vector.tensor_copy(staged[:, 0, :], planes[2][:].indirect(entries(S - TAIL, S)))
-        for lo in range(0, S - TAIL, QUARTER):
-            scalar_gather(3, lo, min(lo + QUARTER, S - TAIL))
-        nc.vector.tensor_copy(staged[:, 1, :], planes[3][:].indirect(entries(S - TAIL, S)))
-        nc.vector.tensor_copy(halves[1][:, HALF - TAIL :, 2:4], staged[:].rearrange("p j t -> p t j"))
+            nc.vector.tensor_copy(picked(HALF, S)[:, :, j], planes[j][:].indirect(entries(HALF, S)))
+        staged = keep.tile([P, 2, V_HI - V_LO], BF16, name="staged", align_bytes=256)
+        for lo, hi in ((0, V_LO), (V_HI, S)):
+            scalar_gather(2, lo, hi)
+        nc.vector.tensor_copy(staged[:, 0, :], planes[2][:].indirect(entries(V_LO, V_HI)))
+        pieces = ((0, 64), (64, 192), (192, 320), (384, 448), (448, 512))
+        for lo, hi in pieces:
+            scalar_gather(3, lo, hi)
+        nc.vector.tensor_copy(staged[:, 1, :], planes[3][:].indirect(entries(V_LO, V_HI)))
+        nc.vector.tensor_copy(picked(V_LO, V_HI)[:, :, 2:4], staged[:].rearrange("p j t -> p t j"))
 
         w_grouped = keep.tile([P, N, PACK], BF16, name="w_grouped", align_bytes=256)
         w_halves = ((0, N // 2), (N // 2, N))
@@ -80,52 +82,57 @@ def tile_picked_pool_lin_bias_sub_e_kernel(tc, xT, w, b, offs, out):
             )
         w_codes = keep.tile([P, N], U32, name="w_codes", align_bytes=256)
         w_scales = keep.tile([P, N], U8, name="w_scales", align_bytes=256)
+        codes = keep.tile([P, S], U32, name="codes", align_bytes=256)
+        early_scales = keep.tile([P, 64], U8, name="early_scales", align_bytes=256)
+        scales = keep.tile([P, S], U8, name="scales", tag="w_raw", align_bytes=256)
 
-        order = (0, 1, 2, 3)
-        codes, scales = {}, {}
-        all_scales = keep.tile([P, S], U8, name="all_scales", tag="w_raw", align_bytes=256)
-        for i, q in enumerate(order):
-            c = keep.tile([P, QUARTER], U32, name="codes%d" % q, align_bytes=256)
-            s = all_scales[:, i * QUARTER : (i + 1) * QUARTER]
-            lo = (q % 2) * QUARTER
-            if i == 0:
-                for wlo, whi in w_halves:
-                    nc.vector.quantize_mx(
-                        out=w_codes[:, wlo:whi].bitcast(FP8X4),
-                        scales=w_scales[:, wlo:whi],
-                        in_=w_grouped[:, wlo:whi, :].rearrange("p n j -> p (n j)"),
-                    )
+        def scale_bytes(lo, hi):
+            return early_scales[:] if lo == 0 else scales[:, lo:hi]
+
+        def quantise_w(lo, hi):
             nc.vector.quantize_mx(
-                out=c[:].bitcast(FP8X4),
-                scales=s,
-                in_=halves[q // 2][:, lo : lo + QUARTER, :].rearrange("p t j -> p (t j)"),
+                out=w_codes[:, lo:hi].bitcast(FP8X4),
+                scales=w_scales[:, lo:hi],
+                in_=w_grouped[:, lo:hi, :].rearrange("p n j -> p (n j)"),
             )
-            codes[q] = c
-            scales[q] = s
 
-        width = QUARTER // D
-        for first, count in ((0, 2), (2, 1), (3, 1)):
-            tag = "picked1" if first == 0 else "best%d" % first
-            best = keep.tile([P, count * width], F32, name="best%d" % first, tag=tag, align_bytes=256)
-            for i in range(count):
-                q = first + i
-                acc = psum.tile([P, QUARTER], F32, name="acc%d" % q)
+        def quantise(lo, hi):
+            nc.vector.quantize_mx(
+                out=codes[:, lo:hi].bitcast(FP8X4),
+                scales=scale_bytes(lo, hi),
+                in_=picked(lo, hi).rearrange("p t j -> p (t j)"),
+            )
+
+        quantise(0, 64)
+        quantise_w(*w_halves[0])
+        quantise_w(*w_halves[1])
+        for lo, hi in ((64, 192), (192, 320), (320, 448), (448, 512)):
+            quantise(lo, hi)
+
+        for passes in (((0, 64), (64, 192)), ((192, 320),), ((320, 448), (448, 512))):
+            first, end = passes[0][0] // D, passes[-1][1] // D
+            best = keep.tile([P, end - first], F32, name="best%d" % first, align_bytes=256)
+            for lo, hi in passes:
+                acc = psum.tile([P, hi - lo], F32, name="acc%d" % lo)
                 nc.tensor.matmul_mx(
                     out=acc[:],
                     lhsT=w_codes[:].bitcast(FP8X4),
                     lhsT_scale=w_scales[:],
-                    rhs=codes[q][:].bitcast(FP8X4),
-                    rhs_scale=scales[q],
+                    rhs=codes[:, lo:hi].bitcast(FP8X4),
+                    rhs_scale=scale_bytes(lo, hi),
                     start=True,
                     stop=True,
                 )
                 nc.vector.tensor_reduce(
-                    best[:, i * width : (i + 1) * width], acc[:].rearrange("m (v d) -> m v d", d=D), axis=X, op=MAX
+                    best[:, lo // D - first : hi // D - first],
+                    acc[:].rearrange("m (v d) -> m v d", d=D),
+                    axis=X,
+                    op=MAX,
                 )
-            result = keep.tile([P, count * width], F32, name="result%d" % first, align_bytes=256)
-            if first == 3:
+            result = keep.tile([P, end - first], F32, name="result%d" % first, align_bytes=256)
+            if end == V:
                 nc.vector.tensor_scalar_add(result[:], best[:], bias[:, 0:1])
             else:
                 nc.scalar.activation(result[:], best[:], IDENTITY, bias=bias[:, 0:1])
-            queue = nc.scalar if first == 2 else nc.sync
-            queue.dma_start(out[:, first * width : (first + count) * width], result[:])
+            queue = nc.sync if first == 0 or end == V else nc.scalar
+            queue.dma_start(out[:, first:end], result[:])

@@ -8,7 +8,8 @@ P = 128
 PACK = 4
 HALF = S // 2
 QUARTER = S // 4
-V_LO, V_HI = 320, 384
+V_HI = 64
+FREE = 128
 FLOPS = 2 * K * S * N
 
 F32 = mybir.dt.float32
@@ -49,77 +50,57 @@ def tile_picked_pool_lin_bias_sub_e_kernel(tc, xT, w, b, offs, out):
         bias = keep.tile([P, 1], F32, name="bias")
         nc.sync.dma_start(bias[:], b)
 
-        gathered = keep.tile([P, S, PACK], BF16, name="gathered", align_bytes=256)
+        grouped = keep.tile([P, N + S, PACK], BF16, name="grouped", align_bytes=256)
+        gathered = grouped[:, N:, :]
 
         def entries(lo, hi):
             return offsets[:, lo // 16 : hi // 16]
 
-        def picked(lo, hi):
-            return gathered[:, lo:hi, :]
-
         def scalar_gather(j, lo, hi):
-            nc.scalar.activation(picked(lo, hi)[:, :, j], planes[j][:].indirect(entries(lo, hi)), COPY)
+            nc.scalar.activation(gathered[:, lo:hi, j], planes[j][:].indirect(entries(lo, hi)), COPY)
 
         for j in range(2):
-            scalar_gather(j, 0, HALF)
-            nc.vector.tensor_copy(picked(HALF, S)[:, :, j], planes[j][:].indirect(entries(HALF, S)))
-        staged = keep.tile([P, 2, V_HI - V_LO], BF16, name="staged", align_bytes=256)
-        for lo, hi in ((0, V_LO), (V_HI, S)):
-            scalar_gather(2, lo, hi)
-        nc.vector.tensor_copy(staged[:, 0, :], planes[2][:].indirect(entries(V_LO, V_HI)))
-        pieces = ((0, 64), (64, 192), (192, 320), (384, 448), (448, 512))
-        for lo, hi in pieces:
+            scalar_gather(j, HALF, S)
+            nc.vector.tensor_copy(gathered[:, 0:HALF, j], planes[j][:].indirect(entries(0, HALF)))
+        staged = keep.tile([P, 2, V_HI], BF16, name="staged", align_bytes=256)
+        scalar_gather(2, V_HI, S)
+        nc.vector.tensor_copy(staged[:, 0, :], planes[2][:].indirect(entries(0, V_HI)))
+        for lo, hi in ((64, 128), (128, 256), (256, 384), (384, 448), (448, 512)):
             scalar_gather(3, lo, hi)
-        nc.vector.tensor_copy(staged[:, 1, :], planes[3][:].indirect(entries(V_LO, V_HI)))
-        nc.vector.tensor_copy(picked(V_LO, V_HI)[:, :, 2:4], staged[:].rearrange("p j t -> p t j"))
+        nc.vector.tensor_copy(staged[:, 1, :], planes[3][:].indirect(entries(0, V_HI)))
+        nc.vector.tensor_copy(gathered[:, 0:V_HI, 2:4], staged[:].rearrange("p j t -> p t j"))
 
-        w_grouped = keep.tile([P, N, PACK], BF16, name="w_grouped", align_bytes=256)
-        w_halves = ((0, N // 2), (N // 2, N))
-        for lo, hi in w_halves:
+        for lo, hi in ((64, 128), (0, 64)):
             nc.vector.tensor_copy(
-                w_grouped[:, lo:hi, :].rearrange("p (c i) j -> p c j i", i=4),
+                grouped[:, lo:hi, :].rearrange("p (c i) j -> p c j i", i=4),
                 w_raw[:, :, lo:hi].rearrange("p j (c i) -> p c j i", i=4),
             )
-        w_codes = keep.tile([P, N], U32, name="w_codes", align_bytes=256)
-        w_scales = keep.tile([P, N], U8, name="w_scales", align_bytes=256)
-        codes = keep.tile([P, S], U32, name="codes", align_bytes=256)
-        early_scales = keep.tile([P, 64], U8, name="early_scales", align_bytes=256)
-        scales = keep.tile([P, S], U8, name="scales", tag="w_raw", align_bytes=256)
+        codes = keep.tile([P, N + S], U32, name="codes", align_bytes=256)
+        free_scales = keep.tile([P, N + FREE], U8, name="free_scales", align_bytes=256)
+        held_scales = keep.tile([P, S - FREE], U8, name="held_scales", tag="w_raw", align_bytes=256)
 
         def scale_bytes(lo, hi):
-            return early_scales[:] if lo == 0 else scales[:, lo:hi]
+            return free_scales[:, lo:hi] if lo < N + FREE else held_scales[:, lo - N - FREE : hi - N - FREE]
 
-        def quantise_w(lo, hi):
-            nc.vector.quantize_mx(
-                out=w_codes[:, lo:hi].bitcast(FP8X4),
-                scales=w_scales[:, lo:hi],
-                in_=w_grouped[:, lo:hi, :].rearrange("p n j -> p (n j)"),
-            )
-
-        def quantise(lo, hi):
+        for lo, hi in ((192, 256), (64, 192), (0, 64), (256, 384), (384, 512), (512, 576), (576, 640)):
             nc.vector.quantize_mx(
                 out=codes[:, lo:hi].bitcast(FP8X4),
                 scales=scale_bytes(lo, hi),
-                in_=picked(lo, hi).rearrange("p t j -> p (t j)"),
+                in_=grouped[:, lo:hi, :].rearrange("p t j -> p (t j)"),
             )
 
-        quantise(0, 64)
-        quantise_w(*w_halves[0])
-        quantise_w(*w_halves[1])
-        for lo, hi in ((64, 192), (192, 320), (320, 448), (448, 512)):
-            quantise(lo, hi)
-
-        for passes in (((0, 64), (64, 192)), ((192, 320),), ((320, 448), (448, 512))):
+        stores = (((0, 128), (128, 256)), ((256, 384),), ((384, 448), (448, 512)))
+        for i, passes in enumerate(stores):
             first, end = passes[0][0] // D, passes[-1][1] // D
             best = keep.tile([P, end - first], F32, name="best%d" % first, align_bytes=256)
             for lo, hi in passes:
                 acc = psum.tile([P, hi - lo], F32, name="acc%d" % lo)
                 nc.tensor.matmul_mx(
                     out=acc[:],
-                    lhsT=w_codes[:].bitcast(FP8X4),
-                    lhsT_scale=w_scales[:],
-                    rhs=codes[:, lo:hi].bitcast(FP8X4),
-                    rhs_scale=scale_bytes(lo, hi),
+                    lhsT=codes[:, 0:N].bitcast(FP8X4),
+                    lhsT_scale=scale_bytes(0, N),
+                    rhs=codes[:, N + lo : N + hi].bitcast(FP8X4),
+                    rhs_scale=scale_bytes(N + lo, N + hi),
                     start=True,
                     stop=True,
                 )
@@ -130,9 +111,9 @@ def tile_picked_pool_lin_bias_sub_e_kernel(tc, xT, w, b, offs, out):
                     op=MAX,
                 )
             result = keep.tile([P, end - first], F32, name="result%d" % first, align_bytes=256)
-            if end == V:
+            if i == 2:
                 nc.vector.tensor_scalar_add(result[:], best[:], bias[:, 0:1])
             else:
                 nc.scalar.activation(result[:], best[:], IDENTITY, bias=bias[:, 0:1])
-            queue = nc.sync if first == 0 or end == V else nc.scalar
+            queue = nc.scalar if i == 1 else nc.sync
             queue.dma_start(out[:, first:end], result[:])

@@ -37,8 +37,8 @@ def tile_picked_pool_lin_bias_sub_e_kernel(tc, xT, w, b, offs, out):
         for j in range(PACK):
             plane = keep.tile([P, T], F32, name="plane%d" % j, align_bytes=256)
             if j < PACK - 1:
-                for lo in (0, T // 2):
-                    nc.sync.dma_start(plane[0:P:2, lo : lo + T // 2], xT_rows[0:P:2, j, lo : lo + T // 2])
+                for first in (0, 2):
+                    nc.sync.dma_start(plane[first:P:4, :], xT_rows[first:P:4, j, :])
                 nc.scalar.dma_start(plane[1:P:2, :], xT_rows[1:P:2, j, :])
             else:
                 nc.sync.dma_start(plane[:], xT_rows[:, j, :])

@@ -33,8 +33,8 @@ def tile_picked_pool_lin_bias_sub_e_kernel(tc, xT, w, b, offs, out):
         offsets = keep.tile([P, S // 16], U16, name="offsets")
 
         xT_rows = xT.rearrange("(p j) t -> p j t", j=PACK)
-        planes = []
-        for j in range(PACK):
+        planes = {}
+        for j in (2, 0, 1, 3):
             plane = keep.tile([P, T], F32, name="plane%d" % j, align_bytes=256)
             if j < PACK - 1:
                 for first in (0, 2):
@@ -42,8 +42,8 @@ def tile_picked_pool_lin_bias_sub_e_kernel(tc, xT, w, b, offs, out):
                 nc.scalar.dma_start(plane[1:P:2, :], xT_rows[1:P:2, j, :])
             else:
                 nc.sync.dma_start(plane[:], xT_rows[:, j, :])
-            planes.append(plane)
-            if j == 0:
+            planes[j] = plane
+            if j == 2:
                 nc.sync.dma_start(offsets[:], offs)
         w_raw = keep.tile([P, PACK, N], F32, name="w_raw", align_bytes=256)
         nc.sync.dma_start(w_raw[:], w.rearrange("(p j) n -> p j n", j=PACK))
@@ -59,12 +59,12 @@ def tile_picked_pool_lin_bias_sub_e_kernel(tc, xT, w, b, offs, out):
         def scalar_gather(j, lo, hi):
             nc.scalar.activation(gathered[:, lo:hi, j], planes[j][:].indirect(entries(lo, hi)), COPY)
 
-        for j in range(2):
-            scalar_gather(j, HALF, S)
-            nc.vector.tensor_copy(gathered[:, 0:HALF, j], planes[j][:].indirect(entries(0, HALF)))
         staged = keep.tile([P, 2, V_HI], BF16, name="staged", align_bytes=256)
         scalar_gather(2, V_HI, S)
         nc.vector.tensor_copy(staged[:, 0, :], planes[2][:].indirect(entries(0, V_HI)))
+        for j in range(2):
+            scalar_gather(j, HALF, S)
+            nc.vector.tensor_copy(gathered[:, 0:HALF, j], planes[j][:].indirect(entries(0, HALF)))
         for lo, hi in ((64, 128), (128, 256), (256, 384), (384, 448), (448, 512)):
             scalar_gather(3, lo, hi)
         nc.vector.tensor_copy(staged[:, 1, :], planes[3][:].indirect(entries(0, V_HI)))

from contextlib import ExitStack

import concourse.mybir as mybir

K, T, S, N, D = 512, 2048, 512, 128, 4
V = S // D
P = 128
PACK = 4
HALF = S // 2
QUARTER = S // 4
V_HI = 64
FREE = 128
FLOPS = 2 * K * S * N

F32 = mybir.dt.float32
BF16 = mybir.dt.bfloat16
U16 = mybir.dt.uint16
U32 = mybir.dt.uint32
U8 = mybir.dt.uint8
FP8X4 = mybir.dt.float8_e4m3fn_x4
MAX = mybir.AluOpType.max
X = mybir.AxisListType.X
IDENTITY = mybir.ActivationFunctionType.Identity
COPY = mybir.ActivationFunctionType.Copy


def tile_picked_pool_lin_bias_sub_e_kernel(tc, xT, w, b, offs, out):
    nc = tc.nc
    with ExitStack() as ctx:
        keep = ctx.enter_context(tc.tile_pool(name="keep", bufs=1))
        psum = ctx.enter_context(tc.psum_pool(name="psum", bufs=1))

        offsets = keep.tile([P, S // 16], U16, name="offsets")

        xT_rows = xT.rearrange("(p j) t -> p j t", j=PACK)
        planes = {}
        for j in (2, 0, 1, 3):
            plane = keep.tile([P, T], F32, name="plane%d" % j, align_bytes=256)
            if j < PACK - 1:
                for first in (0, 2):
                    nc.sync.dma_start(plane[first:P:4, :], xT_rows[first:P:4, j, :])
                nc.scalar.dma_start(plane[1:P:2, :], xT_rows[1:P:2, j, :])
            else:
                nc.sync.dma_start(plane[:], xT_rows[:, j, :])
            planes[j] = plane
            if j == 2:
                nc.sync.dma_start(offsets[:], offs)
        w_raw = keep.tile([P, PACK, N], F32, name="w_raw", align_bytes=256)
        nc.sync.dma_start(w_raw[:], w.rearrange("(p j) n -> p j n", j=PACK))
        bias = keep.tile([P, 1], F32, name="bias")
        nc.sync.dma_start(bias[:], b)

        grouped = keep.tile([P, N + S, PACK], BF16, name="grouped", align_bytes=256)
        gathered = grouped[:, N:, :]

        def entries(lo, hi):
            return offsets[:, lo // 16 : hi // 16]

        def scalar_gather(j, lo, hi):
            nc.scalar.activation(gathered[:, lo:hi, j], planes[j][:].indirect(entries(lo, hi)), COPY)

        staged = keep.tile([P, 2, V_HI], BF16, name="staged", align_bytes=256)
        scalar_gather(2, V_HI, S)
        nc.vector.tensor_copy(staged[:, 0, :], planes[2][:].indirect(entries(0, V_HI)))
        for j in range(2):
            scalar_gather(j, HALF, S)
            nc.vector.tensor_copy(gathered[:, 0:HALF, j], planes[j][:].indirect(entries(0, HALF)))
        for lo, hi in ((64, 128), (128, 256), (256, 384), (384, 448), (448, 512)):
            scalar_gather(3, lo, hi)
        nc.vector.tensor_copy(staged[:, 1, :], planes[3][:].indirect(entries(0, V_HI)))
        nc.vector.tensor_copy(gathered[:, 0:V_HI, 2:4], staged[:].rearrange("p j t -> p t j"))

        for lo, hi in ((64, 128), (0, 64)):
            nc.vector.tensor_copy(
                grouped[:, lo:hi, :].rearrange("p (c i) j -> p c j i", i=4),
                w_raw[:, :, lo:hi].rearrange("p j (c i) -> p c j i", i=4),
            )
        codes = keep.tile([P, N + S], U32, name="codes", align_bytes=256)
        free_scales = keep.tile([P, N + FREE], U8, name="free_scales", align_bytes=256)
        held_scales = keep.tile([P, S - FREE], U8, name="held_scales", tag="w_raw", align_bytes=256)

        def scale_bytes(lo, hi):
            return free_scales[:, lo:hi] if lo < N + FREE else held_scales[:, lo - N - FREE : hi - N - FREE]

        for lo, hi in ((192, 256), (64, 192), (0, 64), (256, 384), (384, 512), (512, 576), (576, 640)):
            nc.vector.quantize_mx(
                out=codes[:, lo:hi].bitcast(FP8X4),
                scales=scale_bytes(lo, hi),
                in_=grouped[:, lo:hi, :].rearrange("p t j -> p (t j)"),
            )

        stores = (((0, 128), (128, 256)), ((256, 384),), ((384, 448), (448, 512)))
        for i, passes in enumerate(stores):
            first, end = passes[0][0] // D, passes[-1][1] // D
            best = keep.tile([P, end - first], F32, name="best%d" % first, align_bytes=256)
            for lo, hi in passes:
                acc = psum.tile([P, hi - lo], F32, name="acc%d" % lo)
                nc.tensor.matmul_mx(
                    out=acc[:],
                    lhsT=codes[:, 0:N].bitcast(FP8X4),
                    lhsT_scale=scale_bytes(0, N),
                    rhs=codes[:, N + lo : N + hi].bitcast(FP8X4),
                    rhs_scale=scale_bytes(N + lo, N + hi),
                    start=True,
                    stop=True,
                )
                nc.vector.tensor_reduce(
                    best[:, lo // D - first : hi // D - first],
                    acc[:].rearrange("m (v d) -> m v d", d=D),
                    axis=X,
                    op=MAX,
                )
            result = keep.tile([P, end - first], F32, name="result%d" % first, align_bytes=256)
            if i == 2:
                nc.vector.tensor_scalar_add(result[:], best[:], bias[:, 0:1])
            else:
                nc.scalar.activation(result[:], best[:], IDENTITY, bias=bias[:, 0:1])
            queue = nc.scalar if i == 1 else nc.sync
            queue.dma_start(out[:, first:end], result[:])
